import numpy as np, ml_dtypes
CORES = [15,47,79,175,207]
N = 5
import mx_ref
NC, G = 256, 4
C = np.float32(0.041)
WID = [192,256,128,192,128]
BF = ml_dtypes.bfloat16
def cut(t, i, w=512):
    return t[:, w * i:w * i + w]
def tile(rs):
    return np.stack(rs, axis=2).reshape(128, -1).astype(BF)
def layer(w, X):
    out = []
    for i in range(G):
        for t in range(len(X)):
            p = mx_ref.matmul(mx_ref.quantize(cut(w, len(X) * i + t)), X[t])
            z = p if t == 0 else z + p
        out.append(z)
    return out
def act(Z):
    return [np.maximum(z, 0) * C for z in Z]
def setup_inputs(rng):
    def f(*shape):
        return mx_ref.flush((rng.standard_normal(shape, dtype=np.float32) * np.exp2(rng.integers(-2, 3, shape[:-1] + (1,)))).astype(BF))
    return {"x": f(N, 128, 4 * NC), "w1": f(N, 128, G * 512), "w2": f(N, 128, 512)}
def setup_inputs_blocks(rng):
    d = setup_inputs(rng)
    for k in ("x", "w1", "w2"): d[k] = mx_ref.spread(d[k], rng, 2)
    return d
def setup_inputs_wide(rng):
    d = setup_inputs(rng)
    for k in ("x", "w1", "w2"): d[k] = mx_ref.flush((d[k].astype(np.float32) * np.exp2(rng.integers(-6, 7, (N, 1, 1))).astype(np.float32)).astype(BF))
    return d
def reference(x, w1, w2):
    X = [mx_ref.quantize(x[j][:, :4 * WID[j]]) for j in range(N)]
    y = np.full((N, 128, NC), np.nan, np.float32)
    for c in range(N):
        for r in range(N):
            p = mx_ref.matmul(mx_ref.quantize(w2[r]), mx_ref.quantize(tile(act(layer(w1[r], [X[c]])))))
            z = p if r == 0 else z + p
        y[c][:, :WID[c]] = z
    return {"y": y}

@@ -1,0 +1,208 @@
+import numpy as np
+from concourse.bass import DstId, RemoteDMATransfer
+from concourse.mybir import dt, AluOpType, ActivationFunctionType
+
+W_ALL = 896
+W_MAX = 256
+G = 4
+NZ = 6
+BANK = 512
+SCALE = float(np.float32(0.041))
+
+SCRATCH = {
+    "xt": ("sbuf", [128, 4 * W_MAX], "bfloat16"),
+    "w1t": ("sbuf", [128, G * 512], "bfloat16"),
+    "w2t": ("sbuf", [128, 512], "bfloat16"),
+    "w1q": ("sbuf", [128, G * 128], "float8_e4m3fn_x4"),
+    "w1s": ("sbuf", [128, G * 128], "uint8"),
+    "w2q": ("sbuf", [128, 128], "float8_e4m3fn_x4"),
+    "w2s": ("sbuf", [128, 128], "uint8"),
+    "xq": ("sbuf", [128, W_ALL], "float8_e4m3fn_x4"),
+    "xs": ("sbuf", [128, W_ALL], "uint8"),
+    "h": ("sbuf", [128, 4 * W_ALL], "bfloat16"),
+    "hq": ("sbuf", [128, W_ALL], "float8_e4m3fn_x4"),
+    "hs": ("sbuf", [128, W_ALL], "uint8"),
+    "res": ("sbuf", [128, W_ALL], "float32"),
+    "land": ("sbuf", [128, 4 * W_MAX], "float32"),
+    "acc": ("sbuf", [128, 4 * W_MAX], "float32"),
+    "z": ("psum", [128, BANK * NZ], "float32"),
+    "p": ("psum", [128, BANK * 2], "float32"),
+}
+SEMAPHORES = (["ldx", "ldwa", "ldwb", "ldw2", "q", "zt", "asc", "avc", "hqd", "pt", "cp", "ad", "st", "sent"]
+              + ["pl%d" % i for i in range(5)] + ["co%d" % i for i in range(5)] + ["rs%d" % i for i in range(5)])
+
+DIRECT = (1, 2)
+RELAY = (3, 4)
+EARLY = (0, 2, 4)
+
+
+def helper_of(core, T, topo):
+    for d in range(256):
+        if (topo.host(d) == topo.host(core) and topo.chip(d) == topo.chip(core) and topo.die(d) != topo.die(core)
+                and topo.may_write(core, d) and T.rank_of(d) is None):
+            return d
+    return None
+
+
+def spread(g, core, topo, dests, src, dsts, remote_sem, local_sem):
+    mask = 0xFFFF
+    ids = []
+    for d in dests:
+        mask &= topo.mask(core, d)
+        rid, pid = topo.addr(d, core)
+        ids.append(DstId(rid=rid, pnc=pid))
+    g.remote_dma_fused([RemoteDMATransfer(dst_ids=ids, dma_engine_mask=mask, remote_sem=remote_sem,
+                                          srcs=[src], dsts=dsts, alu_op=0)], local_sem=local_sem)
+    return bin(mask).count("1")
+
+
+def engines(topo, src, dests):
+    mask = 0xFFFF
+    for d in dests:
+        mask &= topo.mask(src, d)
+    return bin(mask).count("1")
+
+
+def rank_program(g, core, T, topo):
+    wid = T.tables["WID"]
+    n = len(T.cores)
+    off = [sum(wid[:c]) for c in range(n)]
+    helper = [helper_of(T.cores[c], T, topo) for c in range(n)]
+    direct = [[(c + s) % n for s in DIRECT] for c in range(n)]
+    relay = [[(c + s) % n for s in RELAY] for c in range(n)]
+    first = [[helper[c]] + [T.cores[r] for r in direct[c]] for c in range(n)]
+    second = [[T.cores[r] for r in relay[c]] for c in range(n)]
+
+    def codes(buf, c):
+        return T[buf][:, off[c]:off[c] + wid[c]].bitcast(dt.uint8)
+
+    def cols(buf, c):
+        return T[buf][:, off[c]:off[c] + wid[c]]
+
+    rank = T.rank_of(core)
+    if rank is None:
+        if core not in helper:
+            return
+        c = helper.index(core)
+        k = engines(topo, T.cores[c], first[c])
+        g.wait_ge(T.sem["pl%d" % c], k)
+        m = spread(g, core, topo, second[c], cols("xs", c), [cols("xs", c)] * len(second[c]), T.sem["pl%d" % c], T.sem.sent)
+        g.wait_ge(T.sem["co%d" % c], k)
+        m += spread(g, core, topo, second[c], codes("xq", c), [codes("xq", c)] * len(second[c]), T.sem["co%d" % c], T.sem.sent)
+        g.wait_ge(T.sem.sent, m)
+        return
+
+    r = rank
+    w = wid[r]
+    order = [r] + [(r - s) % n for s in DIRECT + RELAY]
+
+    g.sync.dma_start(T.xt[0:64, :4 * w], T.x[0:64, :4 * w]).then_inc(T.sem.ldx, 16)
+    g.scalar.dma_start(T.xt[64:128, :4 * w], T.x[64:128, :4 * w]).then_inc(T.sem.ldx, 16)
+    g.sync.dma_start(T.w1t[:, 0:1024], T.w1[:, 0:1024]).then_inc(T.sem.ldwa, 16)
+    g.scalar.dma_start(T.w1t[:, 1024:2048], T.w1[:, 1024:2048]).then_inc(T.sem.ldwb, 16)
+    g.sync.dma_start(T.w2t[:], T.w2[:]).then_inc(T.sem.ldw2, 16)
+
+    v = g.vector
+    v.wait_ge(T.sem.ldx, 32)
+    v.quantize_mx(T.xq[:, off[r]:off[r] + w], T.xs[:, off[r]:off[r] + w], T.xt[:, :4 * w]).then_inc(T.sem.q, 1)
+    v.wait_ge(T.sem.ldwa, 16)
+    v.quantize_mx(T.w1q[:, 0:256], T.w1s[:, 0:256], T.w1t[:, 0:1024]).then_inc(T.sem.q, 1)
+    v.wait_ge(T.sem.ldwb, 16)
+    v.quantize_mx(T.w1q[:, 256:512], T.w1s[:, 256:512], T.w1t[:, 1024:2048]).then_inc(T.sem.q, 1)
+    v.wait_ge(T.sem.ldw2, 16)
+    v.quantize_mx(T.w2q[:], T.w2s[:], T.w2t[:]).then_inc(T.sem.q, 1)
+
+    g.wait_ge(T.sem.q, 1)
+    sent = spread(g, core, topo, first[r], cols("xs", r), [cols("xs", r)] * len(first[r]), T.sem["pl%d" % r], T.sem.sent)
+    sent += spread(g, core, topo, first[r], codes("xq", r), [codes("xq", r)] * len(first[r]), T.sem["co%d" % r], T.sem.sent)
+
+    def slot(buf, sender, owner):
+        j = (sender - owner - 1) % n
+        return T[buf][:, W_MAX * j:W_MAX * j + wid[owner]]
+
+    for t in range(1, n):
+        c = order[t]
+        g.wait_ge(T.sem.cp, t)
+        sent += spread(g, core, topo, [T.cores[c]], cols("res", c), [slot("land", r, c)], T.sem["rs%d" % r], T.sem.sent)
+    g.wait_ge(T.sem.sent, sent)
+
+    te = g.tensor
+
+    def first_product(t, b):
+        c = order[t]
+        i = G * t + b
+        if t == 0 and b == 0:
+            te.wait_ge(T.sem.q, 2)
+        if t == 0 and b == 2:
+            te.wait_ge(T.sem.q, 3)
+        if t > 0 and b == 0:
+            k = engines(topo, T.cores[c], first[c]) if r in direct[c] else engines(topo, helper[c], second[c])
+            te.wait_ge(T.sem["pl%d" % c], k)
+            te.wait_ge(T.sem["co%d" % c], k)
+        if i >= NZ:
+            te.wait_ge(T.sem.asc if (i - NZ) % 2 == 0 else T.sem.avc, (i - NZ) // 2 + 1)
+        bank = BANK * (i % NZ)
+        te.matmul_mx(T.z[:, bank:bank + wid[c]], T.w1q[:, 128 * b:128 * b + 128], T.w1s[:, 128 * b:128 * b + 128],
+                     cols("xq", c), cols("xs", c), True, True).then_inc(T.sem.zt, 1)
+
+    def second_product(t):
+        c = order[t]
+        if t == 0:
+            te.wait_ge(T.sem.q, 4)
+        te.wait_ge(T.sem.hqd, t + 1)
+        if t > 1:
+            te.wait_ge(T.sem.cp, t - 1)
+        bank = 0 if t == 0 else BANK
+        te.matmul_mx(T.p[:, bank:bank + wid[c]], T.w2q[:], T.w2s[:], cols("hq", c), cols("hs", c), True, True
+                     ).then_inc(T.sem.pt, 1)
+
+    for t in range(n):
+        for b in range(G):
+            first_product(t, b)
+            if b == 1 and t > 0 and t - 1 not in EARLY:
+                second_product(t - 1)
+        if t in EARLY:
+            second_product(t)
+
+    def h_of(c, b):
+        return T.h[:, 4 * off[c] + b:4 * (off[c] + wid[c]):4]
+
+    def z_of(t, b):
+        bank = BANK * ((G * t + b) % NZ)
+        return T.z[:, bank:bank + wid[order[t]]]
+
+    sc = g.scalar
+
+    def take(t):
+        c = order[t]
+        sc.wait_ge(T.sem.pt, t + 1)
+        sc.activation(cols("res", c), T.p[:, BANK:BANK + wid[c]], ActivationFunctionType.Copy).then_inc(T.sem.cp, 1)
+
+    for t in range(n):
+        c = order[t]
+        for b in (0, 2):
+            sc.wait_ge(T.sem.zt, G * t + b + 1)
+            sc.activation(h_of(c, b), z_of(t, b), ActivationFunctionType.Relu, scale=SCALE).then_inc(T.sem.asc, 1)
+            if b == 0 and t > 1 and t - 1 not in EARLY:
+                take(t - 1)
+        if t > 0 and t in EARLY:
+            take(t)
+        for b in (1, 3):
+            v.wait_ge(T.sem.zt, G * t + b + 1)
+            v.tensor_scalar(h_of(c, b), z_of(t, b), 0.0, SCALE, AluOpType.max, AluOpType.mult).then_inc(T.sem.avc, 1)
+        v.wait_ge(T.sem.asc, 2 * (t + 1))
+        v.wait_ge(T.sem.avc, 2 * (t + 1))
+        v.quantize_mx(cols("hq", c), cols("hs", c), T.h[:, 4 * off[c]:4 * (off[c] + wid[c])]).then_inc(T.sem.hqd, 1)
+
+    senders = direct[r] + relay[r]
+    v.wait_ge(T.sem.pt, 1)
+    for j, s in enumerate(senders):
+        v.wait_ge(T.sem["rs%d" % s], engines(topo, T.cores[s], [core]))
+        if j > 0:
+            v.wait_ge(T.sem.ad, j)
+        before = T.p[:, 0:w] if j == 0 else T.acc[:, W_MAX * (j - 1):W_MAX * (j - 1) + w]
+        v.tensor_tensor(T.acc[:, W_MAX * j:W_MAX * j + w], before, slot("land", s, r), AluOpType.add).then_inc(T.sem.ad, 1)
+
+    g.sync.wait_ge(T.sem.ad, len(senders))
+    g.sync.dma_start(T.y[:, :w], T.acc[:, W_MAX * (len(senders) - 1):W_MAX * (len(senders) - 1) + w]).then_inc(T.sem.st, 16)
+    g.sync.wait_ge(T.sem.st, 16)

@@ -4,6 +4,7 @@ from concourse.mybir import dt, AluOpType, ActivationFunctionType
 
 W_ALL = 896
 W_MAX = 256
+W_MIN = 128
 G = 4
 NZ = 6
 BANK = 512
@@ -29,11 +30,13 @@ SCRATCH = {
     "p": ("psum", [128, BANK * 2], "float32"),
 }
 SEMAPHORES = (["ldx", "ldwa", "ldwb", "ldw2", "q", "zt", "asc", "avc", "hqd", "pt", "cp", "ad", "st", "sent"]
-              + ["pl%d" % i for i in range(5)] + ["co%d" % i for i in range(5)] + ["rs%d" % i for i in range(5)])
+              + ["pl%d" % i for i in range(5)] + ["co%d" % i for i in range(5)]
+              + ["rs%d_%d" % (i, j) for i in range(5) for j in range(2)])
 
-DIRECT = (1, 2)
-RELAY = (3, 4)
-EARLY = (0, 2, 4)
+DIRECT = (1, 2, 3)
+RELAY = (4,)
+FEED_WITH = 1
+LATE = (1, 3)
 
 
 def helper_of(core, T, topo):
@@ -44,23 +47,26 @@ def helper_of(core, T, topo):
     return None
 
 
-def spread(g, core, topo, dests, src, dsts, remote_sem, local_sem):
-    mask = 0xFFFF
-    ids = []
-    for d in dests:
-        mask &= topo.mask(core, d)
+def count(mask):
+    return bin(mask).count("1")
+
+
+def feed_mask(core, helper, other, topo):
+    return topo.mask(core, helper) & ~topo.mask(core, other)
+
+
+def pieces_of(width):
+    return [(0, W_MIN), (W_MIN, width)] if width >= 2 * W_MIN else [(0, width)]
+
+
+def write(g, core, topo, pairs, src, dst, remote_sem, local_sem):
+    transfers = []
+    for d, mask in pairs:
         rid, pid = topo.addr(d, core)
-        ids.append(DstId(rid=rid, pnc=pid))
-    g.remote_dma_fused([RemoteDMATransfer(dst_ids=ids, dma_engine_mask=mask, remote_sem=remote_sem,
-                                          srcs=[src], dsts=dsts, alu_op=0)], local_sem=local_sem)
-    return bin(mask).count("1")
-
-
-def engines(topo, src, dests):
-    mask = 0xFFFF
-    for d in dests:
-        mask &= topo.mask(src, d)
-    return bin(mask).count("1")
+        transfers.append(RemoteDMATransfer(dst_ids=[DstId(rid=rid, pnc=pid)], dma_engine_mask=mask, remote_sem=remote_sem,
+                                           srcs=[src], dsts=[dst], alu_op=0))
+    g.remote_dma_fused(transfers, local_sem=local_sem)
+    return sum(count(mask) for d, mask in pairs)
 
 
 def rank_program(g, core, T, topo):
@@ -70,31 +76,39 @@ def rank_program(g, core, T, topo):
     helper = [helper_of(T.cores[c], T, topo) for c in range(n)]
     direct = [[(c + s) % n for s in DIRECT] for c in range(n)]
     relay = [[(c + s) % n for s in RELAY] for c in range(n)]
-    first = [[helper[c]] + [T.cores[r] for r in direct[c]] for c in range(n)]
-    second = [[T.cores[r] for r in relay[c]] for c in range(n)]
+    feed = [feed_mask(T.cores[c], helper[c], T.cores[direct[c][0]], topo) for c in range(n)]
 
     def codes(buf, c):
         return T[buf][:, off[c]:off[c] + wid[c]].bitcast(dt.uint8)
 
-    def cols(buf, c):
-        return T[buf][:, off[c]:off[c] + wid[c]]
+    def cols(buf, c, a=0, b=None):
+        return T[buf][:, off[c] + a:off[c] + (wid[c] if b is None else b)]
 
     rank = T.rank_of(core)
     if rank is None:
         if core not in helper:
             return
         c = helper.index(core)
-        k = engines(topo, T.cores[c], first[c])
-        g.wait_ge(T.sem["pl%d" % c], k)
-        m = spread(g, core, topo, second[c], cols("xs", c), [cols("xs", c)] * len(second[c]), T.sem["pl%d" % c], T.sem.sent)
-        g.wait_ge(T.sem["co%d" % c], k)
-        m += spread(g, core, topo, second[c], codes("xq", c), [codes("xq", c)] * len(second[c]), T.sem["co%d" % c], T.sem.sent)
+        m = 0
+        for r in relay[c]:
+            to = [(T.cores[r], topo.mask(core, T.cores[r]))]
+            g.wait_ge(T.sem["pl%d" % c], count(feed[c]))
+            m += write(g, core, topo, to, cols("xs", c), cols("xs", c), T.sem["pl%d" % c], T.sem.sent)
+            g.wait_ge(T.sem["co%d" % c], count(feed[c]))
+            m += write(g, core, topo, to, codes("xq", c), codes("xq", c), T.sem["co%d" % c], T.sem.sent)
         g.wait_ge(T.sem.sent, m)
         return
 
     r = rank
     w = wid[r]
     order = [r] + [(r - s) % n for s in DIRECT + RELAY]
+    work = [(0, r, 0, w, 0, True)]
+    for t in range(1, n):
+        ps = pieces_of(wid[order[t]])
+        work += [(t, order[t], a, b, j, j == len(ps) - 1) for j, (a, b) in enumerate(ps)]
+
+    def late(u):
+        return u < len(work) - 1 and (not work[u][5] or work[u][0] in LATE)
 
     g.sync.dma_start(T.xt[0:64, :4 * w], T.x[0:64, :4 * w]).then_inc(T.sem.ldx, 16)
     g.scalar.dma_start(T.xt[64:128, :4 * w], T.x[64:128, :4 * w]).then_inc(T.sem.ldx, 16)
@@ -104,7 +118,7 @@ def rank_program(g, core, T, topo):
 
     v = g.vector
     v.wait_ge(T.sem.ldx, 32)
-    v.quantize_mx(T.xq[:, off[r]:off[r] + w], T.xs[:, off[r]:off[r] + w], T.xt[:, :4 * w]).then_inc(T.sem.q, 1)
+    v.quantize_mx(cols("xq", r), cols("xs", r), T.xt[:, :4 * w]).then_inc(T.sem.q, 1)
     v.wait_ge(T.sem.ldwa, 16)
     v.quantize_mx(T.w1q[:, 0:256], T.w1s[:, 0:256], T.w1t[:, 0:1024]).then_inc(T.sem.q, 1)
     v.wait_ge(T.sem.ldwb, 16)
@@ -113,96 +127,103 @@ def rank_program(g, core, T, topo):
     v.quantize_mx(T.w2q[:], T.w2s[:], T.w2t[:]).then_inc(T.sem.q, 1)
 
     g.wait_ge(T.sem.q, 1)
-    sent = spread(g, core, topo, first[r], cols("xs", r), [cols("xs", r)] * len(first[r]), T.sem["pl%d" % r], T.sem.sent)
-    sent += spread(g, core, topo, first[r], codes("xq", r), [codes("xq", r)] * len(first[r]), T.sem["co%d" % r], T.sem.sent)
+    sent = 0
+    for k, d in enumerate(direct[r]):
+        to = [(T.cores[d], topo.mask(core, T.cores[d]))]
+        if k == FEED_WITH:
+            to = [(helper[r], feed[r])] + to
+        sent += write(g, core, topo, to, cols("xs", r), cols("xs", r), T.sem["pl%d" % r], T.sem.sent)
+        sent += write(g, core, topo, to, codes("xq", r), codes("xq", r), T.sem["co%d" % r], T.sem.sent)
 
-    def slot(buf, sender, owner):
+    def slot(buf, sender, owner, a, b):
         j = (sender - owner - 1) % n
-        return T[buf][:, W_MAX * j:W_MAX * j + wid[owner]]
+        return T[buf][:, W_MAX * j + a:W_MAX * j + b]
 
-    for t in range(1, n):
-        c = order[t]
-        g.wait_ge(T.sem.cp, t)
-        sent += spread(g, core, topo, [T.cores[c]], cols("res", c), [slot("land", r, c)], T.sem["rs%d" % r], T.sem.sent)
+    for u in range(1, len(work)):
+        t, c, a, b, j, last = work[u]
+        g.wait_ge(T.sem.cp, u)
+        sent += write(g, core, topo, [(T.cores[c], topo.mask(core, T.cores[c]))], cols("res", c, a, b), slot("land", r, c, a, b),
+                      T.sem["rs%d_%d" % (r, j)], T.sem.sent)
     g.wait_ge(T.sem.sent, sent)
 
     te = g.tensor
 
-    def first_product(t, b):
-        c = order[t]
-        i = G * t + b
-        if t == 0 and b == 0:
+    def first_product(u, k):
+        t, c, a, b, j, last = work[u]
+        i = G * u + k
+        if u == 0 and k == 0:
             te.wait_ge(T.sem.q, 2)
-        if t == 0 and b == 2:
+        if u == 0 and k == 2:
             te.wait_ge(T.sem.q, 3)
-        if t > 0 and b == 0:
-            k = engines(topo, T.cores[c], first[c]) if r in direct[c] else engines(topo, helper[c], second[c])
-            te.wait_ge(T.sem["pl%d" % c], k)
-            te.wait_ge(T.sem["co%d" % c], k)
+        if t > 0 and j == 0 and k == 0:
+            m = count(topo.mask(T.cores[c] if r in direct[c] else helper[c], core))
+            te.wait_ge(T.sem["pl%d" % c], m)
+            te.wait_ge(T.sem["co%d" % c], m)
         if i >= NZ:
             te.wait_ge(T.sem.asc if (i - NZ) % 2 == 0 else T.sem.avc, (i - NZ) // 2 + 1)
         bank = BANK * (i % NZ)
-        te.matmul_mx(T.z[:, bank:bank + wid[c]], T.w1q[:, 128 * b:128 * b + 128], T.w1s[:, 128 * b:128 * b + 128],
-                     cols("xq", c), cols("xs", c), True, True).then_inc(T.sem.zt, 1)
+        te.matmul_mx(T.z[:, bank:bank + b - a], T.w1q[:, 128 * k:128 * k + 128], T.w1s[:, 128 * k:128 * k + 128],
+                     cols("xq", c, a, b), cols("xs", c, a, b), True, True).then_inc(T.sem.zt, 1)
 
-    def second_product(t):
-        c = order[t]
-        if t == 0:
+    def second_product(u):
+        t, c, a, b, j, last = work[u]
+        if u == 0:
             te.wait_ge(T.sem.q, 4)
-        te.wait_ge(T.sem.hqd, t + 1)
-        if t > 1:
-            te.wait_ge(T.sem.cp, t - 1)
-        bank = 0 if t == 0 else BANK
-        te.matmul_mx(T.p[:, bank:bank + wid[c]], T.w2q[:], T.w2s[:], cols("hq", c), cols("hs", c), True, True
+        te.wait_ge(T.sem.hqd, u + 1)
+        if u > 1:
+            te.wait_ge(T.sem.cp, u - 1)
+        bank = 0 if u == 0 else BANK
+        te.matmul_mx(T.p[:, bank:bank + b - a], T.w2q[:], T.w2s[:], cols("hq", c, a, b), cols("hs", c, a, b), True, True
                      ).then_inc(T.sem.pt, 1)
 
-    for t in range(n):
-        for b in range(G):
-            first_product(t, b)
-            if b == 1 and t > 0 and t - 1 not in EARLY:
-                second_product(t - 1)
-        if t in EARLY:
-            second_product(t)
-
-    def h_of(c, b):
-        return T.h[:, 4 * off[c] + b:4 * (off[c] + wid[c]):4]
-
-    def z_of(t, b):
-        bank = BANK * ((G * t + b) % NZ)
-        return T.z[:, bank:bank + wid[order[t]]]
+    for u in range(len(work)):
+        for k in range(G):
+            first_product(u, k)
+        if u > 0 and late(u - 1):
+            second_product(u - 1)
+        if not late(u):
+            second_product(u)
 
     sc = g.scalar
 
-    def take(t):
-        c = order[t]
-        sc.wait_ge(T.sem.pt, t + 1)
-        sc.activation(cols("res", c), T.p[:, BANK:BANK + wid[c]], ActivationFunctionType.Copy).then_inc(T.sem.cp, 1)
+    def take(u):
+        t, c, a, b, j, last = work[u]
+        sc.wait_ge(T.sem.pt, u + 1)
+        sc.activation(cols("res", c, a, b), T.p[:, BANK:BANK + b - a], ActivationFunctionType.Copy).then_inc(T.sem.cp, 1)
 
-    for t in range(n):
-        c = order[t]
-        for b in (0, 2):
-            sc.wait_ge(T.sem.zt, G * t + b + 1)
-            sc.activation(h_of(c, b), z_of(t, b), ActivationFunctionType.Relu, scale=SCALE).then_inc(T.sem.asc, 1)
-            if b == 0 and t > 1 and t - 1 not in EARLY:
-                take(t - 1)
-        if t > 0 and t in EARLY:
-            take(t)
-        for b in (1, 3):
-            v.wait_ge(T.sem.zt, G * t + b + 1)
-            v.tensor_scalar(h_of(c, b), z_of(t, b), 0.0, SCALE, AluOpType.max, AluOpType.mult).then_inc(T.sem.avc, 1)
-        v.wait_ge(T.sem.asc, 2 * (t + 1))
-        v.wait_ge(T.sem.avc, 2 * (t + 1))
-        v.quantize_mx(cols("hq", c), cols("hs", c), T.h[:, 4 * off[c]:4 * (off[c] + wid[c])]).then_inc(T.sem.hqd, 1)
+    for u in range(len(work)):
+        t, c, a, b, j, last = work[u]
+        lo, hi = 4 * (off[c] + a), 4 * (off[c] + b)
+        z = [T.z[:, BANK * ((G * u + k) % NZ):BANK * ((G * u + k) % NZ) + b - a] for k in range(G)]
+        for k in (0, 2):
+            sc.wait_ge(T.sem.zt, G * u + k + 1)
+            sc.activation(T.h[:, lo + k:hi:4], z[k], ActivationFunctionType.Relu, scale=SCALE).then_inc(T.sem.asc, 1)
+        if u > 1 and late(u - 1):
+            take(u - 1)
+        if u > 0 and not late(u):
+            take(u)
+        for k in (1, 3):
+            v.wait_ge(T.sem.zt, G * u + k + 1)
+            v.tensor_scalar(T.h[:, lo + k:hi:4], z[k], 0.0, SCALE, AluOpType.max, AluOpType.mult).then_inc(T.sem.avc, 1)
+        v.wait_ge(T.sem.asc, 2 * (u + 1))
+        v.wait_ge(T.sem.avc, 2 * (u + 1))
+        v.quantize_mx(cols("hq", c, a, b), cols("hs", c, a, b), T.h[:, lo:hi]).then_inc(T.sem.hqd, 1)
 
     senders = direct[r] + relay[r]
+    mine = pieces_of(w)
+    done = [0]
     v.wait_ge(T.sem.pt, 1)
-    for j, s in enumerate(senders):
-        v.wait_ge(T.sem["rs%d" % s], engines(topo, T.cores[s], [core]))
-        if j > 0:
-            v.wait_ge(T.sem.ad, j)
-        before = T.p[:, 0:w] if j == 0 else T.acc[:, W_MAX * (j - 1):W_MAX * (j - 1) + w]
-        v.tensor_tensor(T.acc[:, W_MAX * j:W_MAX * j + w], before, slot("land", s, r), AluOpType.add).then_inc(T.sem.ad, 1)
+    for i, s in enumerate(senders):
+        for j, (a, b) in enumerate(mine):
+            v.wait_ge(T.sem["rs%d_%d" % (s, j)], count(topo.mask(T.cores[s], core)))
+            if i > 0:
+                v.wait_ge(T.sem.ad, len(mine) * (i - 1) + j + 1)
+            before = T.p[:, a:b] if i == 0 else T.acc[:, W_MAX * (i - 1) + a:W_MAX * (i - 1) + b]
+            v.tensor_tensor(T.acc[:, W_MAX * i + a:W_MAX * i + b], before, slot("land", s, r, a, b), AluOpType.add
+                            ).then_inc(T.sem.ad, 1)
 
-    g.sync.wait_ge(T.sem.ad, len(senders))
-    g.sync.dma_start(T.y[:, :w], T.acc[:, W_MAX * (len(senders) - 1):W_MAX * (len(senders) - 1) + w]).then_inc(T.sem.st, 16)
-    g.sync.wait_ge(T.sem.st, 16)
+    i = len(senders) - 1
+    for j, (a, b) in enumerate(mine):
+        g.sync.wait_ge(T.sem.ad, len(mine) * i + j + 1)
+        g.sync.dma_start(T.y[:, a:b], T.acc[:, W_MAX * i + a:W_MAX * i + b]).then_inc(T.sem.st, 16)
+    g.sync.wait_ge(T.sem.st, 16 * len(mine))

import numpy as np
from concourse.bass import DstId, RemoteDMATransfer
from concourse.mybir import dt, AluOpType, ActivationFunctionType

W_ALL = 896
W_MAX = 256
W_MIN = 128
G = 4
NZ = 6
BANK = 512
SCALE = float(np.float32(0.041))

SCRATCH = {
    "xt": ("sbuf", [128, 4 * W_MAX], "bfloat16"),
    "w1t": ("sbuf", [128, G * 512], "bfloat16"),
    "w2t": ("sbuf", [128, 512], "bfloat16"),
    "w1q": ("sbuf", [128, G * 128], "float8_e4m3fn_x4"),
    "w1s": ("sbuf", [128, G * 128], "uint8"),
    "w2q": ("sbuf", [128, 128], "float8_e4m3fn_x4"),
    "w2s": ("sbuf", [128, 128], "uint8"),
    "xq": ("sbuf", [128, W_ALL], "float8_e4m3fn_x4"),
    "xs": ("sbuf", [128, W_ALL], "uint8"),
    "h": ("sbuf", [128, 4 * W_ALL], "bfloat16"),
    "hq": ("sbuf", [128, W_ALL], "float8_e4m3fn_x4"),
    "hs": ("sbuf", [128, W_ALL], "uint8"),
    "res": ("sbuf", [128, W_ALL], "float32"),
    "land": ("sbuf", [128, 4 * W_MAX], "float32"),
    "acc": ("sbuf", [128, 4 * W_MAX], "float32"),
    "z": ("psum", [128, BANK * NZ], "float32"),
    "p": ("psum", [128, BANK * 2], "float32"),
}
SEMAPHORES = (["ldx", "ldwa", "ldwb", "ldw2", "q", "zt", "asc", "avc", "hqd", "pt", "cp", "ad", "st", "sent"]
              + ["pl%d" % i for i in range(5)] + ["co%d" % i for i in range(5)]
              + ["rs%d_%d" % (i, j) for i in range(5) for j in range(2)])

DIRECT = (1, 2, 3)
RELAY = (4,)
FEED_WITH = 1
LATE = (1, 3)


def helper_of(core, T, topo):
    for d in range(256):
        if (topo.host(d) == topo.host(core) and topo.chip(d) == topo.chip(core) and topo.die(d) != topo.die(core)
                and topo.may_write(core, d) and T.rank_of(d) is None):
            return d
    return None


def count(mask):
    return bin(mask).count("1")


def feed_mask(core, helper, other, topo):
    return topo.mask(core, helper) & ~topo.mask(core, other)


def pieces_of(width):
    return [(0, W_MIN), (W_MIN, width)] if width >= 2 * W_MIN else [(0, width)]


def write(g, core, topo, pairs, src, dst, remote_sem, local_sem):
    transfers = []
    for d, mask in pairs:
        rid, pid = topo.addr(d, core)
        transfers.append(RemoteDMATransfer(dst_ids=[DstId(rid=rid, pnc=pid)], dma_engine_mask=mask, remote_sem=remote_sem,
                                           srcs=[src], dsts=[dst], alu_op=0))
    g.remote_dma_fused(transfers, local_sem=local_sem)
    return sum(count(mask) for d, mask in pairs)


def rank_program(g, core, T, topo):
    wid = T.tables["WID"]
    n = len(T.cores)
    off = [sum(wid[:c]) for c in range(n)]
    helper = [helper_of(T.cores[c], T, topo) for c in range(n)]
    direct = [[(c + s) % n for s in DIRECT] for c in range(n)]
    relay = [[(c + s) % n for s in RELAY] for c in range(n)]
    feed = [feed_mask(T.cores[c], helper[c], T.cores[direct[c][0]], topo) for c in range(n)]

    def codes(buf, c):
        return T[buf][:, off[c]:off[c] + wid[c]].bitcast(dt.uint8)

    def cols(buf, c, a=0, b=None):
        return T[buf][:, off[c] + a:off[c] + (wid[c] if b is None else b)]

    rank = T.rank_of(core)
    if rank is None:
        if core not in helper:
            return
        c = helper.index(core)
        m = 0
        for r in relay[c]:
            to = [(T.cores[r], topo.mask(core, T.cores[r]))]
            g.wait_ge(T.sem["pl%d" % c], count(feed[c]))
            m += write(g, core, topo, to, cols("xs", c), cols("xs", c), T.sem["pl%d" % c], T.sem.sent)
            g.wait_ge(T.sem["co%d" % c], count(feed[c]))
            m += write(g, core, topo, to, codes("xq", c), codes("xq", c), T.sem["co%d" % c], T.sem.sent)
        g.wait_ge(T.sem.sent, m)
        return

    r = rank
    w = wid[r]
    order = [r] + [(r - s) % n for s in DIRECT + RELAY]
    work = [(0, r, 0, w, 0, True)]
    for t in range(1, n):
        ps = pieces_of(wid[order[t]])
        work += [(t, order[t], a, b, j, j == len(ps) - 1) for j, (a, b) in enumerate(ps)]

    def late(u):
        return u < len(work) - 1 and (not work[u][5] or work[u][0] in LATE)

    g.sync.dma_start(T.xt[0:64, :4 * w], T.x[0:64, :4 * w]).then_inc(T.sem.ldx, 16)
    g.scalar.dma_start(T.xt[64:128, :4 * w], T.x[64:128, :4 * w]).then_inc(T.sem.ldx, 16)
    g.sync.dma_start(T.w1t[:, 0:1024], T.w1[:, 0:1024]).then_inc(T.sem.ldwa, 16)
    g.scalar.dma_start(T.w1t[:, 1024:2048], T.w1[:, 1024:2048]).then_inc(T.sem.ldwb, 16)
    g.sync.dma_start(T.w2t[:], T.w2[:]).then_inc(T.sem.ldw2, 16)

    v = g.vector
    v.wait_ge(T.sem.ldx, 32)
    v.quantize_mx(cols("xq", r), cols("xs", r), T.xt[:, :4 * w]).then_inc(T.sem.q, 1)
    v.wait_ge(T.sem.ldwa, 16)
    v.quantize_mx(T.w1q[:, 0:256], T.w1s[:, 0:256], T.w1t[:, 0:1024]).then_inc(T.sem.q, 1)
    v.wait_ge(T.sem.ldwb, 16)
    v.quantize_mx(T.w1q[:, 256:512], T.w1s[:, 256:512], T.w1t[:, 1024:2048]).then_inc(T.sem.q, 1)
    v.wait_ge(T.sem.ldw2, 16)
    v.quantize_mx(T.w2q[:], T.w2s[:], T.w2t[:]).then_inc(T.sem.q, 1)

    g.wait_ge(T.sem.q, 1)
    sent = 0
    for k, d in enumerate(direct[r]):
        to = [(T.cores[d], topo.mask(core, T.cores[d]))]
        if k == FEED_WITH:
            to = [(helper[r], feed[r])] + to
        sent += write(g, core, topo, to, cols("xs", r), cols("xs", r), T.sem["pl%d" % r], T.sem.sent)
        sent += write(g, core, topo, to, codes("xq", r), codes("xq", r), T.sem["co%d" % r], T.sem.sent)

    def slot(buf, sender, owner, a, b):
        j = (sender - owner - 1) % n
        return T[buf][:, W_MAX * j + a:W_MAX * j + b]

    for u in range(1, len(work)):
        t, c, a, b, j, last = work[u]
        g.wait_ge(T.sem.cp, u)
        sent += write(g, core, topo, [(T.cores[c], topo.mask(core, T.cores[c]))], cols("res", c, a, b), slot("land", r, c, a, b),
                      T.sem["rs%d_%d" % (r, j)], T.sem.sent)
    g.wait_ge(T.sem.sent, sent)

    te = g.tensor

    def first_product(u, k):
        t, c, a, b, j, last = work[u]
        i = G * u + k
        if u == 0 and k == 0:
            te.wait_ge(T.sem.q, 2)
        if u == 0 and k == 2:
            te.wait_ge(T.sem.q, 3)
        if t > 0 and j == 0 and k == 0:
            m = count(topo.mask(T.cores[c] if r in direct[c] else helper[c], core))
            te.wait_ge(T.sem["pl%d" % c], m)
            te.wait_ge(T.sem["co%d" % c], m)
        if i >= NZ:
            te.wait_ge(T.sem.asc if (i - NZ) % 2 == 0 else T.sem.avc, (i - NZ) // 2 + 1)
        bank = BANK * (i % NZ)
        te.matmul_mx(T.z[:, bank:bank + b - a], T.w1q[:, 128 * k:128 * k + 128], T.w1s[:, 128 * k:128 * k + 128],
                     cols("xq", c, a, b), cols("xs", c, a, b), True, True).then_inc(T.sem.zt, 1)

    def second_product(u):
        t, c, a, b, j, last = work[u]
        if u == 0:
            te.wait_ge(T.sem.q, 4)
        te.wait_ge(T.sem.hqd, u + 1)
        if u > 1:
            te.wait_ge(T.sem.cp, u - 1)
        bank = 0 if u == 0 else BANK
        te.matmul_mx(T.p[:, bank:bank + b - a], T.w2q[:], T.w2s[:], cols("hq", c, a, b), cols("hs", c, a, b), True, True
                     ).then_inc(T.sem.pt, 1)

    for u in range(len(work)):
        for k in range(G):
            first_product(u, k)
        if u > 0 and late(u - 1):
            second_product(u - 1)
        if not late(u):
            second_product(u)

    sc = g.scalar

    def take(u):
        t, c, a, b, j, last = work[u]
        sc.wait_ge(T.sem.pt, u + 1)
        sc.activation(cols("res", c, a, b), T.p[:, BANK:BANK + b - a], ActivationFunctionType.Copy).then_inc(T.sem.cp, 1)

    for u in range(len(work)):
        t, c, a, b, j, last = work[u]
        lo, hi = 4 * (off[c] + a), 4 * (off[c] + b)
        z = [T.z[:, BANK * ((G * u + k) % NZ):BANK * ((G * u + k) % NZ) + b - a] for k in range(G)]
        for k in (0, 2):
            sc.wait_ge(T.sem.zt, G * u + k + 1)
            sc.activation(T.h[:, lo + k:hi:4], z[k], ActivationFunctionType.Relu, scale=SCALE).then_inc(T.sem.asc, 1)
        if u > 1 and late(u - 1):
            take(u - 1)
        if u > 0 and not late(u):
            take(u)
        for k in (1, 3):
            v.wait_ge(T.sem.zt, G * u + k + 1)
            v.tensor_scalar(T.h[:, lo + k:hi:4], z[k], 0.0, SCALE, AluOpType.max, AluOpType.mult).then_inc(T.sem.avc, 1)
        v.wait_ge(T.sem.asc, 2 * (u + 1))
        v.wait_ge(T.sem.avc, 2 * (u + 1))
        v.quantize_mx(cols("hq", c, a, b), cols("hs", c, a, b), T.h[:, lo:hi]).then_inc(T.sem.hqd, 1)

    senders = direct[r] + relay[r]
    mine = pieces_of(w)
    done = [0]
    v.wait_ge(T.sem.pt, 1)
    for i, s in enumerate(senders):
        for j, (a, b) in enumerate(mine):
            v.wait_ge(T.sem["rs%d_%d" % (s, j)], count(topo.mask(T.cores[s], core)))
            if i > 0:
                v.wait_ge(T.sem.ad, len(mine) * (i - 1) + j + 1)
            before = T.p[:, a:b] if i == 0 else T.acc[:, W_MAX * (i - 1) + a:W_MAX * (i - 1) + b]
            v.tensor_tensor(T.acc[:, W_MAX * i + a:W_MAX * i + b], before, slot("land", s, r, a, b), AluOpType.add
                            ).then_inc(T.sem.ad, 1)

    i = len(senders) - 1
    for j, (a, b) in enumerate(mine):
        g.sync.wait_ge(T.sem.ad, len(mine) * i + j + 1)
        g.sync.dma_start(T.y[:, a:b], T.acc[:, W_MAX * i + a:W_MAX * i + b]).then_inc(T.sem.st, 16)
    g.sync.wait_ge(T.sem.st, 16 * len(mine))
